import numpy as np, ml_dtypes
CORES = [71,199,95,223,103,231,111,239,119,247,127,255]
N = 12
TK = 256
def setup_inputs(rng):
    return {"x": rng.standard_normal((N, 128, TK), dtype=np.float32).astype(ml_dtypes.bfloat16), "w": rng.standard_normal((N, 128, 128), dtype=np.float32).astype(ml_dtypes.bfloat16)}
def setup_inputs_big(rng):
    d = setup_inputs(rng)
    for k in ("x", "w"): d[k] = (d[k].astype(np.float32) * 1024.0).astype(d[k].dtype)
    return d
def setup_inputs_small(rng):
    d = setup_inputs(rng)
    for k in ("x", "w"): d[k] = (d[k].astype(np.float32) * (1 / 1024.0)).astype(d[k].dtype)
    return d
def setup_inputs_apart(rng):
    d = setup_inputs(rng)
    f = (10.0 ** rng.permutation(np.linspace(-1.5, 1.5, N))).astype(np.float32).reshape(N, 1, 1)
    for k in ("x", "w"): d[k] = (d[k].astype(np.float32) * f).astype(d[k].dtype)
    return d
def setup_inputs_neg(rng):
    d = setup_inputs(rng)
    d["x"] = (np.abs(d["x"].astype(np.float32)) * 1048576.0).astype(d["x"].dtype); d["w"] = (-np.abs(d["w"].astype(np.float32))).astype(d["w"].dtype)
    return d
def reference(x, w):
    X, W = x.astype(np.float64), w.astype(np.float64)
    y = np.stack([np.max([W[j].T @ X[r] for j in range(N)], axis=0) for r in range(N)])
    return {"y": y.astype(ml_dtypes.bfloat16)}

@@ -1,0 +1,130 @@
+from concourse.bass import DstId, RemoteDMATransfer
+from concourse.mybir import AluOpType
+
+N = 12
+M = 128
+TK = 256
+GROUPS = [("d", [1, 2, 3]), ("d", [4, 5, 6]), ("d", [7, 8, 9]), ("s", [10, 11])]
+TAKE = [0, 3, 1, 2]
+NBANK = 8
+
+SCRATCH = {
+    "wd": ("dram", [128, M], "bfloat16"),
+    "gd": ("dram", [N, 128, M], "bfloat16"),
+    "wall": ("sbuf", [128, N * M], "bfloat16"),
+    "xs": ("sbuf", [128, TK], "bfloat16"),
+    "acc0": ("sbuf", [128, TK], "bfloat16"),
+    "acc1": ("sbuf", [128, TK], "bfloat16"),
+}
+for _b in range(NBANK):
+    SCRATCH["ps%d" % _b] = ("psum", [128, 512], "float32")
+
+SEMAPHORES = (["wdl", "w0l", "xl", "sent", "stored"] + ["arr%d" % i for i in range(len(GROUPS))]
+              + ["ld%d" % p for p in range(N)] + ["mm%d" % n for n in range(N)] + ["vv%d" % n for n in range(N)])
+
+
+def _planes(cores, topo):
+    classes = []
+    for r, c in enumerate(cores):
+        for cl in classes:
+            if topo.same_plane(cores[cl[0]], c):
+                cl.append(r)
+                break
+        else:
+            classes.append([r])
+    return classes
+
+
+def _order(rank, cores, topo):
+    classes = _planes(cores, topo)
+    own = [cl for cl in classes if rank in cl][0]
+    i = own.index(rank)
+    order = [rank] + [own[(i + k) % len(own)] for k in range(1, len(own))]
+    for cl in classes:
+        if cl is not own:
+            order += [cl[(i + k) % len(cl)] for k in range(len(cl))]
+    return order
+
+
+def rank_program(g, core, T, topo):
+    rank = T.rank_of(core)
+    if rank is None:
+        return
+    cores = list(T.cores)
+    order = _order(rank, cores, topo)
+    S = T.sem
+
+    def slot(p):
+        return T.wall[:, p * M:(p + 1) * M]
+
+    g.sync.dma_start(T.wd[:], T.w[:]).then_inc(S.wdl, 16)
+    g.scalar.dma_start(slot(0), T.w[:]).then_inc(S.w0l, 16)
+    g.scalar.dma_start(T.xs[:], T.x[:]).then_inc(S.xl, 16)
+
+    sent = 0
+    neng = {}
+    seen = set()
+    for gi, (kind, pos) in enumerate(GROUPS):
+        dsts = [cores[order[p]] for p in pos]
+        mask = topo.mask(core, dsts[0])
+        for d in dsts:
+            mask &= topo.mask(core, d)
+        k = bin(mask).count("1")
+        neng[gi] = k
+        ids = []
+        for d in dsts:
+            rid, pid = topo.addr(d, core)
+            ids.append(DstId(rid=rid, pnc=pid))
+        if kind not in seen:
+            seen.add(kind)
+            g.wait_ge(S.wdl if kind == "d" else S.w0l, 16)
+        g.remote_dma_fused([RemoteDMATransfer(
+            dst_ids=ids, dma_engine_mask=mask, remote_sem=S["arr%d" % gi],
+            srcs=[T.wd[:] if kind == "d" else slot(0)],
+            dsts=[T.gd[p] if kind == "d" else slot(p) for p in pos], alu_op=0)], local_sem=S.sent)
+        sent += k
+
+    queues = [g.sync, g.scalar]
+    nq = 0
+    for gi, (kind, pos) in enumerate(GROUPS):
+        if kind != "d":
+            continue
+        waited = set()
+        for p in pos:
+            q = queues[nq % 2]
+            if nq % 2 not in waited:
+                waited.add(nq % 2)
+                q.wait_ge(S["arr%d" % gi], neng[gi] * len(pos))
+            q.dma_start(slot(p), T.gd[p]).then_inc(S["ld%d" % p], 16)
+            nq += 1
+
+    seq = [(None, 0)]
+    for gi in TAKE:
+        seq += [(gi, p) for p in GROUPS[gi][1]]
+    acc = [T.acc0, T.acc1]
+    g.tensor.wait_ge(S.w0l, 16)
+    g.tensor.wait_ge(S.xl, 16)
+    direct_waited = set()
+    for n, (gi, p) in enumerate(seq):
+        if gi is not None:
+            if GROUPS[gi][0] == "d":
+                g.tensor.wait_ge(S["ld%d" % p], 16)
+            elif gi not in direct_waited:
+                direct_waited.add(gi)
+                g.tensor.wait_ge(S["arr%d" % gi], neng[gi] * len(GROUPS[gi][1]))
+        if n >= NBANK:
+            g.tensor.wait_ge(S["vv%d" % (n - NBANK)], 1)
+        ps = T["ps%d" % (n % NBANK)][:, 0:TK]
+        g.tensor.matmul(ps, slot(p), T.xs[:], True, True).then_inc(S["mm%d" % n], 1)
+
+        g.vector.wait_ge(S["mm%d" % n], 1)
+        if n == 0:
+            g.vector.tensor_copy(acc[0][:], ps).then_inc(S.vv0, 1)
+        else:
+            g.vector.wait_ge(S["vv%d" % (n - 1)], 1)
+            g.vector.tensor_tensor(acc[n % 2][:], ps, acc[(n - 1) % 2][:], AluOpType.max).then_inc(S["vv%d" % n], 1)
+
+    g.sync.wait_ge(S["vv%d" % (N - 1)], 1)
+    g.sync.dma_start(T.y[:], acc[(N - 1) % 2][:]).then_inc(S.stored, 16)
+    g.sync.wait_ge(S.stored, 16)
+    g.wait_ge(S.sent, sent)

@@ -4,13 +4,10 @@ from concourse.mybir import AluOpType
 N = 12
 M = 128
 TK = 256
-GROUPS = [("d", [1, 2, 3]), ("d", [4, 5, 6]), ("d", [7, 8, 9]), ("s", [10, 11])]
-TAKE = [0, 3, 1, 2]
+GROUPS = [[1, 2, 3, 4], [5, 6, 7, 8], [9, 10], [11]]
 NBANK = 8
 
 SCRATCH = {
-    "wd": ("dram", [128, M], "bfloat16"),
-    "gd": ("dram", [N, 128, M], "bfloat16"),
     "wall": ("sbuf", [128, N * M], "bfloat16"),
     "xs": ("sbuf", [128, TK], "bfloat16"),
     "acc0": ("sbuf", [128, TK], "bfloat16"),
@@ -19,8 +16,8 @@ SCRATCH = {
 for _b in range(NBANK):
     SCRATCH["ps%d" % _b] = ("psum", [128, 512], "float32")
 
-SEMAPHORES = (["wdl", "w0l", "xl", "sent", "stored"] + ["arr%d" % i for i in range(len(GROUPS))]
-              + ["ld%d" % p for p in range(N)] + ["mm%d" % n for n in range(N)] + ["vv%d" % n for n in range(N)])
+SEMAPHORES = (["w0l", "xl", "sent", "stored"] + ["arr%d" % i for i in range(len(GROUPS))]
+              + ["mm%d" % n for n in range(N)] + ["vv%d" % n for n in range(N)])
 
 
 def _planes(cores, topo):
@@ -57,61 +54,38 @@ def rank_program(g, core, T, topo):
     def slot(p):
         return T.wall[:, p * M:(p + 1) * M]
 
-    g.sync.dma_start(T.wd[:], T.w[:]).then_inc(S.wdl, 16)
-    g.scalar.dma_start(slot(0), T.w[:]).then_inc(S.w0l, 16)
+    g.sync.dma_start(slot(0), T.w[:]).then_inc(S.w0l, 16)
     g.scalar.dma_start(T.xs[:], T.x[:]).then_inc(S.xl, 16)
 
+    g.wait_ge(S.w0l, 16)
     sent = 0
     neng = {}
-    seen = set()
-    for gi, (kind, pos) in enumerate(GROUPS):
+    for gi, pos in enumerate(GROUPS):
         dsts = [cores[order[p]] for p in pos]
         mask = topo.mask(core, dsts[0])
         for d in dsts:
             mask &= topo.mask(core, d)
-        k = bin(mask).count("1")
-        neng[gi] = k
+        neng[gi] = bin(mask).count("1")
         ids = []
         for d in dsts:
             rid, pid = topo.addr(d, core)
             ids.append(DstId(rid=rid, pnc=pid))
-        if kind not in seen:
-            seen.add(kind)
-            g.wait_ge(S.wdl if kind == "d" else S.w0l, 16)
         g.remote_dma_fused([RemoteDMATransfer(
             dst_ids=ids, dma_engine_mask=mask, remote_sem=S["arr%d" % gi],
-            srcs=[T.wd[:] if kind == "d" else slot(0)],
-            dsts=[T.gd[p] if kind == "d" else slot(p) for p in pos], alu_op=0)], local_sem=S.sent)
-        sent += k
-
-    queues = [g.sync, g.scalar]
-    nq = 0
-    for gi, (kind, pos) in enumerate(GROUPS):
-        if kind != "d":
-            continue
-        waited = set()
-        for p in pos:
-            q = queues[nq % 2]
-            if nq % 2 not in waited:
-                waited.add(nq % 2)
-                q.wait_ge(S["arr%d" % gi], neng[gi] * len(pos))
-            q.dma_start(slot(p), T.gd[p]).then_inc(S["ld%d" % p], 16)
-            nq += 1
+            srcs=[slot(0)], dsts=[slot(p) for p in pos], alu_op=0)], local_sem=S.sent)
+        sent += neng[gi]
 
     seq = [(None, 0)]
-    for gi in TAKE:
-        seq += [(gi, p) for p in GROUPS[gi][1]]
+    for gi, pos in enumerate(GROUPS):
+        seq += [(gi, p) for p in pos]
     acc = [T.acc0, T.acc1]
     g.tensor.wait_ge(S.w0l, 16)
     g.tensor.wait_ge(S.xl, 16)
-    direct_waited = set()
+    waited = set()
     for n, (gi, p) in enumerate(seq):
-        if gi is not None:
-            if GROUPS[gi][0] == "d":
-                g.tensor.wait_ge(S["ld%d" % p], 16)
-            elif gi not in direct_waited:
-                direct_waited.add(gi)
-                g.tensor.wait_ge(S["arr%d" % gi], neng[gi] * len(GROUPS[gi][1]))
+        if gi is not None and gi not in waited:
+            waited.add(gi)
+            g.tensor.wait_ge(S["arr%d" % gi], neng[gi] * len(GROUPS[gi]))
         if n >= NBANK:
             g.tensor.wait_ge(S["vv%d" % (n - NBANK)], 1)
         ps = T["ps%d" % (n % NBANK)][:, 0:TK]

@@ -4,7 +4,7 @@ from concourse.mybir import AluOpType
 N = 12
 M = 128
 TK = 256
-GROUPS = [[1, 2, 3, 4], [5, 6, 7, 8], [9, 10], [11]]
+GROUPS = [[p] for p in range(1, N)]
 NBANK = 8
 
 SCRATCH = {

from concourse.bass import DstId, RemoteDMATransfer
from concourse.mybir import AluOpType

N = 12
M = 128
TK = 256
GROUPS = [[p] for p in range(1, N)]
NBANK = 8

SCRATCH = {
    "wall": ("sbuf", [128, N * M], "bfloat16"),
    "xs": ("sbuf", [128, TK], "bfloat16"),
    "acc0": ("sbuf", [128, TK], "bfloat16"),
    "acc1": ("sbuf", [128, TK], "bfloat16"),
}
for _b in range(NBANK):
    SCRATCH["ps%d" % _b] = ("psum", [128, 512], "float32")

SEMAPHORES = (["w0l", "xl", "sent", "stored"] + ["arr%d" % i for i in range(len(GROUPS))]
              + ["mm%d" % n for n in range(N)] + ["vv%d" % n for n in range(N)])


def _planes(cores, topo):
    classes = []
    for r, c in enumerate(cores):
        for cl in classes:
            if topo.same_plane(cores[cl[0]], c):
                cl.append(r)
                break
        else:
            classes.append([r])
    return classes


def _order(rank, cores, topo):
    classes = _planes(cores, topo)
    own = [cl for cl in classes if rank in cl][0]
    i = own.index(rank)
    order = [rank] + [own[(i + k) % len(own)] for k in range(1, len(own))]
    for cl in classes:
        if cl is not own:
            order += [cl[(i + k) % len(cl)] for k in range(len(cl))]
    return order


def rank_program(g, core, T, topo):
    rank = T.rank_of(core)
    if rank is None:
        return
    cores = list(T.cores)
    order = _order(rank, cores, topo)
    S = T.sem

    def slot(p):
        return T.wall[:, p * M:(p + 1) * M]

    g.sync.dma_start(slot(0), T.w[:]).then_inc(S.w0l, 16)
    g.scalar.dma_start(T.xs[:], T.x[:]).then_inc(S.xl, 16)

    g.wait_ge(S.w0l, 16)
    sent = 0
    neng = {}
    for gi, pos in enumerate(GROUPS):
        dsts = [cores[order[p]] for p in pos]
        mask = topo.mask(core, dsts[0])
        for d in dsts:
            mask &= topo.mask(core, d)
        neng[gi] = bin(mask).count("1")
        ids = []
        for d in dsts:
            rid, pid = topo.addr(d, core)
            ids.append(DstId(rid=rid, pnc=pid))
        g.remote_dma_fused([RemoteDMATransfer(
            dst_ids=ids, dma_engine_mask=mask, remote_sem=S["arr%d" % gi],
            srcs=[slot(0)], dsts=[slot(p) for p in pos], alu_op=0)], local_sem=S.sent)
        sent += neng[gi]

    seq = [(None, 0)]
    for gi, pos in enumerate(GROUPS):
        seq += [(gi, p) for p in pos]
    acc = [T.acc0, T.acc1]
    g.tensor.wait_ge(S.w0l, 16)
    g.tensor.wait_ge(S.xl, 16)
    waited = set()
    for n, (gi, p) in enumerate(seq):
        if gi is not None and gi not in waited:
            waited.add(gi)
            g.tensor.wait_ge(S["arr%d" % gi], neng[gi] * len(GROUPS[gi]))
        if n >= NBANK:
            g.tensor.wait_ge(S["vv%d" % (n - NBANK)], 1)
        ps = T["ps%d" % (n % NBANK)][:, 0:TK]
        g.tensor.matmul(ps, slot(p), T.xs[:], True, True).then_inc(S["mm%d" % n], 1)

        g.vector.wait_ge(S["mm%d" % n], 1)
        if n == 0:
            g.vector.tensor_copy(acc[0][:], ps).then_inc(S.vv0, 1)
        else:
            g.vector.wait_ge(S["vv%d" % (n - 1)], 1)
            g.vector.tensor_tensor(acc[n % 2][:], ps, acc[(n - 1) % 2][:], AluOpType.max).then_inc(S["vv%d" % n], 1)

    g.sync.wait_ge(S["vv%d" % (N - 1)], 1)
    g.sync.dma_start(T.y[:], acc[(N - 1) % 2][:]).then_inc(S.stored, 16)
    g.sync.wait_ge(S.stored, 16)
    g.wait_ge(S.sent, sent)
